import numpy as np
import ml_dtypes


def mxq(x, axis, fmt="e4m3"):
    dtype, down = {"e4m3": (ml_dtypes.float8_e4m3fn, 7), "e5m2": (ml_dtypes.float8_e5m2, 14)}[fmt]
    v = np.moveaxis(np.asarray(x, np.float32).astype(ml_dtypes.bfloat16).astype(np.float64), axis, -1)
    blocks = v.reshape(v.shape[:-1] + (-1, 32))
    amax = np.abs(blocks).max(-1, keepdims=True)
    byte = np.maximum(np.where(amax > 0, np.frexp(amax)[1] - 1 + 127, 0) - down, 1)
    scale = np.exp2(byte - 127.0)
    codes = (blocks / scale).astype(np.float32).astype(dtype).astype(np.float64)
    return np.moveaxis((codes * scale).reshape(v.shape), -1, axis)


WIDE = False


def mx_kscale(k, group=512):
    if not WIDE:
        return np.ones(k)
    levels = np.array([10, -10, 5, -5, 0])
    if group != 512:
        return np.exp2(np.random.permutation(np.resize(levels, k // group))).repeat(group)
    if k % 512:
        return np.exp2(np.random.permutation(np.resize(levels, k // 32))).repeat(32)
    a = np.empty((k // 512, 16))
    for p in range(k // 512):
        a[p, :8] = np.random.permutation(np.resize(levels, 8))
        for g in range(8):
            far = levels[np.abs(levels - a[p, g]) >= 10]
            a[p, g + 8] = far[np.random.randint(len(far))]
    return np.exp2(a.ravel()).repeat(32)


def f64(x):
    return np.asarray(x).astype(np.float64)


def striped(idx):
    return np.tile(np.asarray(idx).reshape(-1, 16).T, (8, 1)).astype(np.uint16)


def unstriped(offs):
    return offs[:16].T.reshape(-1).astype(np.int64)


H, KV, D, NQ, N = 4, 4, 128, 512, 1024


def setup_inputs():
    n = np.random.standard_normal
    s = mx_kscale(D, 0)[:, None]
    u = mx_kscale(N)
    t = np.random.uniform(0.5, 2.0, N) * u
    v = n((KV, N, 128))
    v[:, :, 127] = 1.0
    return {
        "qT": (n((H, D, NQ)) * s * (0.70 / np.sqrt(D))).astype(np.float32),
        "kT": (n((KV, D, N)) / s).astype(np.float32),
        "t": t.reshape(N, 1).astype(np.float32),
        "v": (v / t[:, None]).astype(np.float32),
        "kb": (0.5 * n((N, 1))).astype(np.float32),
        "sink": (N * np.random.uniform(0.1, 1.0, (H, NQ, 1))).astype(np.float32),
    }


def reference(qT, kT, t, v, kb, sink):
    a = mxq(f64(kT), 1, "e4m3").transpose(0, 2, 1) @ mxq(f64(qT), 1, "e4m3")
    a = a + f64(kb)
    p = np.exp(a)
    w = p * f64(t)
    y = mxq(w, 1, "e4m3").transpose(0, 2, 1) @ mxq(f64(v), 1, "e4m3")
    y = y / (y[:, :, 127:128] + f64(sink))
    return y

@@ -1,0 +1,250 @@
+from contextlib import ExitStack
+
+import concourse.mybir as mybir
+
+H, D, NQ, N = 4, 128, 512, 1024
+FLOPS = 2 * 2 * H * NQ * N * D
+
+F32 = mybir.dt.float32
+BF16 = mybir.dt.bfloat16
+I32 = mybir.dt.int32
+U32 = mybir.dt.uint32
+U8 = mybir.dt.uint8
+FP8X4 = mybir.dt.float8_e4m3fn_x4
+ACT = mybir.ActivationFunctionType
+ALU = mybir.AluOpType
+
+P = 128
+PACK = 4
+ROWS = 32
+PASSES = N // (P * PACK)
+QB = NQ // P
+LN2 = 0.6931471805599453
+
+
+def tile_rows_a_exp_kb_sink_kernel(tc, qT, kT, t, v, kb, sink, out):
+    nc = tc.nc
+    with ExitStack() as ctx:
+        sb = ctx.enter_context(tc.tile_pool(name="sb", bufs=1))
+        ps = ctx.enter_context(tc.psum_pool(name="ps", bufs=1))
+        ctx.enter_context(tc.manual_schedule())
+
+        def sbuf(name, shape, dtype):
+            return sb.tile(shape, dtype, name=name, align_bytes=64)
+
+        def planes(name, width):
+            return sbuf(name + "_c", [P, width], U32), sbuf(name + "_s", [P, width], U8)
+
+        def quantize(dst, src):
+            nc.vector.quantize_mx(out=dst[0][:].bitcast(FP8X4), scales=dst[1][:], in_=src[:])
+
+        t_sb = sbuf("t_sb", [P, PASSES * PACK], F32)
+        kb_sb = sbuf("kb_sb", [P, PASSES * PACK], F32)
+        nc.scalar.dma_start(out=t_sb[:].rearrange("p (g j) -> p g j", g=PASSES),
+                            in_=t.rearrange("(g p j) o -> p g (j o)", g=PASSES, j=PACK))
+        nc.scalar.dma_start(out=kb_sb[:].rearrange("p (g j) -> p g j", g=PASSES),
+                            in_=kb.rearrange("(g p j) o -> p g (j o)", g=PASSES, j=PACK))
+        q_raw = sbuf("q_raw", [P, PACK, NQ], F32)
+        nc.sync.dma_start(out=q_raw[:], in_=qT.rearrange("h (p j) n -> (h p) j n", j=PACK))
+        k_view = kT.rearrange("h (p j) n -> (h p) j n", j=PACK)
+        k_raw = []
+        for g in range(PASSES):
+            k_raw.append(sbuf("k_raw%d" % g, [P, PACK, 512], F32))
+            nc.sync.dma_start(out=k_raw[g][:], in_=k_view[:, :, 512 * g: 512 * (g + 1)])
+        v_raw = []
+        for h in range(H):
+            v_raw.append(sbuf("v_raw%d" % h, [P, PASSES, PACK * D], F32))
+            nc.sync.dma_start(out=v_raw[h][:], in_=v[h].rearrange("(g p j) e -> p g (j e)", g=PASSES, j=PACK))
+        sink_sb = sbuf("sink_sb", [P, H, QB], F32)
+        nc.sync.dma_start(out=sink_sb[:], in_=sink.rearrange("h (p b) o -> p h (b o)", b=QB))
+
+        W8 = PASSES * PACK
+        pow2 = sbuf("pow2", [P, W8], I32)
+        expo = sbuf("expo", [P, W8], I32)
+        inv = sbuf("inv", [P, W8], F32)
+        mant = sbuf("mant", [P, W8], F32)
+        b0 = sbuf("b0", [P, W8], F32)
+        b1 = sbuf("b1", [P, W8], F32)
+        ln_m = sbuf("ln_m", [P, W8], F32)
+        bias = sbuf("bias", [P, W8], F32)
+        sgn = sbuf("sgn", [P, W8], BF16)
+        t_bits = t_sb[:].bitcast(I32)
+        nc.vector.tensor_scalar(out=pow2[:], in0=t_bits, scalar1=-(1 << 23), scalar2=None, op0=ALU.bitwise_and)
+        nc.vector.tensor_scalar(out=expo[:], in0=t_bits, scalar1=23, scalar2=255,
+                                op0=ALU.logical_shift_right, op1=ALU.bitwise_and)
+        nc.vector.reciprocal(out=inv[:], in_=pow2[:].bitcast(F32))
+        nc.vector.tensor_scalar(out=b0[:], in0=expo[:], scalar1=-127.0, scalar2=LN2, op0=ALU.add, op1=ALU.mult)
+        nc.vector.tensor_tensor(out=mant[:], in0=t_sb[:], in1=inv[:], op=ALU.mult)
+        nc.vector.tensor_tensor(out=b1[:], in0=b0[:], in1=kb_sb[:], op=ALU.add)
+        nc.scalar.activation(out=ln_m[:], in_=mant[:], func=ACT.Ln)
+        nc.scalar.activation(out=sgn[:], in_=t_sb[:], func=ACT.Sign)
+
+        def deal_pair(name, raw, pair):
+            dst = sbuf(name, [P, 2 * P * PACK], BF16)
+            nc.vector.tensor_copy(
+                out=dst[:].rearrange("p (r s j) -> p s j r", r=2, j=PACK),
+                in_=raw[:].rearrange("p j (s r) -> p s j r", r=PACK)[:, :, :, 2 * pair: 2 * pair + 2])
+            return dst
+
+        q_mx = [planes("q%d" % i, 2 * P) for i in range(2)]
+        k_mx = [[planes("k%d%d" % (g, i), 2 * P) for i in range(2)] for g in range(PASSES)]
+        q_bf = [deal_pair("q_bf%d" % i, q_raw, i) for i in range(2)]
+        for i in range(2):
+            quantize(q_mx[i], q_bf[i])
+        ka = deal_pair("k_bf00", k_raw[0], 0)
+        nc.vector.tensor_tensor(out=bias[:], in0=b1[:], in1=ln_m[:], op=ALU.add)
+        quantize(k_mx[0][0], ka)
+        kb_bf = deal_pair("k_bf01", k_raw[0], 1)
+        quantize(k_mx[0][1], kb_bf)
+
+        def prep_k1():
+            bf = [deal_pair("k_bf1%d" % i, k_raw[1], i) for i in range(2)]
+            for i in range(2):
+                quantize(k_mx[1][i], bf[i])
+
+        v_mx = [planes("v%d" % h, PASSES * D) for h in range(H)]
+        v_bf = [sbuf("v_bf%d" % h, [P, PASSES * D * PACK], BF16) for h in range(H)]
+        v_sg = [sbuf("v_sg%d" % h, [P, PASSES * D * PACK], BF16) for h in range(H)]
+
+        def v_copy(h, copy):
+            for g in range(PASSES):
+                copy(out=v_bf[h][:, 512 * g: 512 * (g + 1)].rearrange("p (c i j) -> p c j i", i=4, j=PACK),
+                     in_=v_raw[h][:, g, :].rearrange("p (j c i) -> p c j i", j=PACK, i=4))
+
+        def v_sign(h):
+            nc.vector.tensor_tensor(
+                out=v_sg[h][:].rearrange("p (g e j) -> p g e j", g=PASSES, j=PACK),
+                in0=v_bf[h][:].rearrange("p (g e j) -> p g e j", g=PASSES, j=PACK),
+                in1=sgn[:].rearrange("p (g j) -> p g j", g=PASSES).unsqueeze(2).to_broadcast([P, PASSES, D, PACK]),
+                op=ALU.mult)
+
+        TILES = PASSES * H
+        banks = [[ps.tile([P, NQ], F32, name="s%d%d" % (h, i)) for i in range(2 if h in (0, H - 1) else 1)]
+                 for h in range(H)]
+        y_bank = [ps.tile([P, NQ], F32, name="y%d" % i) for i in range(2)]
+        w_rows = [sbuf("w_rows%d" % k, [P, PACK, NQ], BF16) for k in range(TILES)]
+        w_int = [sbuf("w_int%d" % i, [P, 2 * P * PACK], BF16) for i in range(4)]
+        w_mx = [[planes("w%d%d" % (k, i), 2 * P) for i in range(2)] for k in range(TILES)]
+        steps = sorted([(k, r) for k in range(TILES) for r in range(PACK)], key=lambda kr: 4 * kr[0] + 3 * kr[1])
+
+        def bank_of(k, r):
+            own = banks[k % H]
+            return own[r % len(own)]
+
+        def scores(k, r):
+            g, h = divmod(k, H)
+            rows = slice(ROWS * h, ROWS * (h + 1))
+            kc, ks = k_mx[g][r // 2]
+            kcol = slice(P * (r % 2), P * (r % 2 + 1))
+            for b in range(QB):
+                qc, qs = q_mx[b // 2]
+                qcol = slice(P * (b % 2), P * (b % 2 + 1))
+                nc.tensor.matmul_mx(out=bank_of(k, r)[:, P * b: P * (b + 1)],
+                                    lhsT=kc[rows, kcol].bitcast(FP8X4), lhsT_scale=ks[rows, kcol],
+                                    rhs=qc[rows, qcol].bitcast(FP8X4), rhs_scale=qs[rows, qcol],
+                                    start=True, stop=True)
+
+        def weights(k, r):
+            col = (k // H) * PACK + r
+            nc.scalar.activation(out=w_rows[k][:, r, :], in_=bank_of(k, r)[:], func=ACT.Exp,
+                                 bias=bias[:, col: col + 1])
+
+        def w_copy(k, i):
+            nc.vector.tensor_copy(
+                out=w_int[2 * (k % 2) + i][:].rearrange("p (c i r) -> p c r i", i=4, r=PACK),
+                in_=w_rows[k][:, :, 2 * P * i: 2 * P * (i + 1)].rearrange("p r (c i) -> p c r i", i=4))
+
+        def w_quant(k, i):
+            quantize(w_mx[k][i], w_int[2 * (k % 2) + i])
+
+        def pv(h, blocks, bank):
+            for b in blocks:
+                for g in range(PASSES):
+                    wc, ws = w_mx[g * H + h][b // 2]
+                    wcol = slice(P * (b % 2), P * (b % 2 + 1))
+                    vcol = slice(D * g, D * (g + 1))
+                    nc.tensor.matmul_mx(out=bank[:, D * b: D * (b + 1)],
+                                        lhsT=wc[:, wcol].bitcast(FP8X4), lhsT_scale=ws[:, wcol],
+                                        rhs=v_mx[h][0][:, vcol].bitcast(FP8X4), rhs_scale=v_mx[h][1][:, vcol],
+                                        start=(g == 0), stop=(g == PASSES - 1))
+
+        parts = [(0, 0, 4, 0), (1, 0, 4, 1), (2, 0, 4, 0), (3, 0, 2, 1), (3, 2, 4, 0)]
+        den = [sbuf("den%d" % i, [P, QB], F32) for i in range(len(parts))]
+        rec = [sbuf("rec%d" % i, [P, QB], F32) for i in range(len(parts))]
+        res = [sbuf("res%d" % i, [P, QB, D], F32) for i in range(len(parts))]
+
+        def part_pv(i):
+            h, lo, hi, bk = parts[i]
+            pv(h, range(lo, hi), y_bank[bk])
+
+        def part_den(i):
+            h, lo, hi, bk = parts[i]
+            y = y_bank[bk][:].rearrange("p (b e) -> p b e", e=D)
+            nc.vector.tensor_tensor(out=den[i][:, lo:hi], in0=y[:, lo:hi, D - 1], in1=sink_sb[:, h, lo:hi], op=ALU.add)
+
+        def part_rec(i):
+            h, lo, hi, bk = parts[i]
+            nc.vector.reciprocal(out=rec[i][:, lo:hi], in_=den[i][:, lo:hi])
+
+        def part_store(i):
+            h, lo, hi, bk = parts[i]
+            nc.sync.dma_start(out=out[h].rearrange("(p b) e -> p b e", b=QB)[:, lo:hi, :], in_=res[i][:, lo:hi, :])
+
+        def part_scale_scalar(i):
+            h, lo, hi, bk = parts[i]
+            for b in range(lo, hi):
+                nc.scalar.activation(out=res[i][:, b, :], in_=y_bank[bk][:, D * b: D * (b + 1)], func=ACT.Copy,
+                                     scale=rec[i][:, b: b + 1])
+            part_store(i)
+
+        def part_scale_vector(i):
+            h, lo, hi, bk = parts[i]
+            y = y_bank[bk][:].rearrange("p (b e) -> p b e", e=D)
+            nc.vector.tensor_tensor(out=res[i][:, lo:hi, :], in0=y[:, lo:hi, :],
+                                    in1=rec[i][:, lo:hi].unsqueeze(2).to_broadcast([P, hi - lo, D]), op=ALU.mult)
+            part_store(i)
+
+        SCALAR_V = H - 1
+        prep_k1()
+        v_copy(0, nc.vector.tensor_copy)
+        v_sign(0)
+        AHEAD = 2
+        for n in range(AHEAD):
+            scores(*steps[n])
+        for n, (k, r) in enumerate(steps):
+            weights(k, r)
+            if n + AHEAD < len(steps):
+                scores(*steps[n + AHEAD])
+            if n == 12:
+                v_copy(SCALAR_V, nc.scalar.copy)
+            if r == PACK - 1 and k < H:
+                w_copy(k, 0)
+                quantize(v_mx[k], v_sg[k])
+                w_copy(k, 1)
+                w_quant(k, 0)
+                if k + 1 < H and k + 1 != SCALAR_V:
+                    v_copy(k + 1, nc.vector.tensor_copy)
+                w_quant(k, 1)
+                if k + 1 < H:
+                    v_sign(k + 1)
+        for k in range(H, TILES):
+            h = k - H
+            w_copy(k, 0)
+            w_copy(k, 1)
+            if h > 0:
+                part_den(h - 1)
+            w_quant(k, 0)
+            if h > 0:
+                part_rec(h - 1)
+                part_scale_scalar(h - 1)
+            w_quant(k, 1)
+            if h < H - 1:
+                part_pv(h)
+        part_pv(3)
+        part_pv(4)
+        part_den(3)
+        part_rec(3)
+        part_scale_scalar(3)
+        part_den(4)
+        part_rec(4)
+        part_scale_vector(4)

@@ -40,21 +40,28 @@ def tile_rows_a_exp_kb_sink_kernel(tc, qT, kT, t, v, kb, sink, out):
 
         t_sb = sbuf("t_sb", [P, PASSES * PACK], F32)
         kb_sb = sbuf("kb_sb", [P, PASSES * PACK], F32)
-        nc.scalar.dma_start(out=t_sb[:].rearrange("p (g j) -> p g j", g=PASSES),
+        nc.sync.dma_start(out=t_sb[:].rearrange("p (g j) -> p g j", g=PASSES),
                             in_=t.rearrange("(g p j) o -> p g (j o)", g=PASSES, j=PACK))
         nc.scalar.dma_start(out=kb_sb[:].rearrange("p (g j) -> p g j", g=PASSES),
                             in_=kb.rearrange("(g p j) o -> p g (j o)", g=PASSES, j=PACK))
         q_raw = sbuf("q_raw", [P, PACK, NQ], F32)
         nc.sync.dma_start(out=q_raw[:], in_=qT.rearrange("h (p j) n -> (h p) j n", j=PACK))
         k_view = kT.rearrange("h (p j) n -> (h p) j n", j=PACK)
-        k_raw = []
-        for g in range(PASSES):
-            k_raw.append(sbuf("k_raw%d" % g, [P, PACK, 512], F32))
+        k_raw = [sbuf("k_raw%d" % g, [P, PACK, 512], F32) for g in range(PASSES)]
+        v_raw = [sbuf("v_raw%d" % h, [P, PASSES, PACK * D], F32) for h in range(H)]
+
+        def load_k(g):
             nc.sync.dma_start(out=k_raw[g][:], in_=k_view[:, :, 512 * g: 512 * (g + 1)])
-        v_raw = []
-        for h in range(H):
-            v_raw.append(sbuf("v_raw%d" % h, [P, PASSES, PACK * D], F32))
+
+        def load_v(h):
             nc.sync.dma_start(out=v_raw[h][:], in_=v[h].rearrange("(g p j) e -> p g (j e)", g=PASSES, j=PACK))
+
+        load_k(0)
+        load_v(0)
+        load_v(1)
+        load_k(1)
+        load_v(2)
+        load_v(3)
         sink_sb = sbuf("sink_sb", [P, H, QB], F32)
         nc.sync.dma_start(out=sink_sb[:], in_=sink.rearrange("h (p b) o -> p h (b o)", b=QB))
 
@@ -75,7 +82,6 @@ def tile_rows_a_exp_kb_sink_kernel(tc, qT, kT, t, v, kb, sink, out):
         nc.vector.reciprocal(out=inv[:], in_=pow2[:].bitcast(F32))
         nc.vector.tensor_scalar(out=b0[:], in0=expo[:], scalar1=-127.0, scalar2=LN2, op0=ALU.add, op1=ALU.mult)
         nc.vector.tensor_tensor(out=mant[:], in0=t_sb[:], in1=inv[:], op=ALU.mult)
-        nc.vector.tensor_tensor(out=b1[:], in0=b0[:], in1=kb_sb[:], op=ALU.add)
         nc.scalar.activation(out=ln_m[:], in_=mant[:], func=ACT.Ln)
         nc.scalar.activation(out=sgn[:], in_=t_sb[:], func=ACT.Sign)
 
@@ -89,27 +95,22 @@ def tile_rows_a_exp_kb_sink_kernel(tc, qT, kT, t, v, kb, sink, out):
         q_mx = [planes("q%d" % i, 2 * P) for i in range(2)]
         k_mx = [[planes("k%d%d" % (g, i), 2 * P) for i in range(2)] for g in range(PASSES)]
         q_bf = [deal_pair("q_bf%d" % i, q_raw, i) for i in range(2)]
-        for i in range(2):
-            quantize(q_mx[i], q_bf[i])
+        quantize(q_mx[0], q_bf[0])
+        nc.vector.tensor_tensor(out=b1[:], in0=b0[:], in1=kb_sb[:], op=ALU.add)
+        quantize(q_mx[1], q_bf[1])
         ka = deal_pair("k_bf00", k_raw[0], 0)
         nc.vector.tensor_tensor(out=bias[:], in0=b1[:], in1=ln_m[:], op=ALU.add)
         quantize(k_mx[0][0], ka)
         kb_bf = deal_pair("k_bf01", k_raw[0], 1)
-        quantize(k_mx[0][1], kb_bf)
-
-        def prep_k1():
-            bf = [deal_pair("k_bf1%d" % i, k_raw[1], i) for i in range(2)]
-            for i in range(2):
-                quantize(k_mx[1][i], bf[i])
 
         v_mx = [planes("v%d" % h, PASSES * D) for h in range(H)]
         v_bf = [sbuf("v_bf%d" % h, [P, PASSES * D * PACK], BF16) for h in range(H)]
         v_sg = [sbuf("v_sg%d" % h, [P, PASSES * D * PACK], BF16) for h in range(H)]
 
-        def v_copy(h, copy):
-            for g in range(PASSES):
-                copy(out=v_bf[h][:, 512 * g: 512 * (g + 1)].rearrange("p (c i j) -> p c j i", i=4, j=PACK),
-                     in_=v_raw[h][:, g, :].rearrange("p (j c i) -> p c j i", j=PACK, i=4))
+        def v_copy(h):
+            nc.vector.tensor_copy(
+                out=v_bf[h][:].rearrange("p (g c i j) -> p g c j i", g=PASSES, i=4, j=PACK),
+                in_=v_raw[h][:].rearrange("p g (j c i) -> p g c j i", j=PACK, i=4))
 
         def v_sign(h):
             nc.vector.tensor_tensor(
@@ -119,30 +120,38 @@ def tile_rows_a_exp_kb_sink_kernel(tc, qT, kT, t, v, kb, sink, out):
                 op=ALU.mult)
 
         TILES = PASSES * H
-        banks = [[ps.tile([P, NQ], F32, name="s%d%d" % (h, i)) for i in range(2 if h in (0, H - 1) else 1)]
+        banks = [[ps.tile([P, NQ], F32, name="s%d%d" % (h, i)) for i in range(2 if h == H - 1 else 1)]
                  for h in range(H)]
-        y_bank = [ps.tile([P, NQ], F32, name="y%d" % i) for i in range(2)]
+        y_bank = [ps.tile([P, NQ], F32, name="y%d" % i) for i in range(3)]
         w_rows = [sbuf("w_rows%d" % k, [P, PACK, NQ], BF16) for k in range(TILES)]
-        w_int = [sbuf("w_int%d" % i, [P, 2 * P * PACK], BF16) for i in range(4)]
-        w_mx = [[planes("w%d%d" % (k, i), 2 * P) for i in range(2)] for k in range(TILES)]
-        steps = sorted([(k, r) for k in range(TILES) for r in range(PACK)], key=lambda kr: 4 * kr[0] + 3 * kr[1])
+        pieces = [[(0, 2), (2, 4)]] * (TILES - 1) + [[(0, 2), (2, 3), (3, 4)]]
+        w_int = [[sbuf("w_int%d%d" % (k, i), [P, (hi - lo) * P * PACK], BF16) for i, (lo, hi) in enumerate(pieces[k])]
+                 for k in range(TILES)]
+        w_mx = [[planes("w%d%d" % (k, i), (hi - lo) * P) for i, (lo, hi) in enumerate(pieces[k])]
+                for k in range(TILES)]
+        left = sorted([(k, r) for k in range(TILES) for r in range(PACK)], key=lambda kr: 4 * kr[0] + 3 * kr[1])
+        steps = []
+        for n in range(len(left)):
+            recent = [k % H for k, r in steps[-2:]]
+            step = ([kr for kr in left if kr[0] % H not in recent] + left)[0]
+            steps.append(step)
+            left.remove(step)
 
         def bank_of(k, r):
             own = banks[k % H]
             return own[r % len(own)]
 
-        def scores(k, r):
+        def score(k, r, b):
             g, h = divmod(k, H)
             rows = slice(ROWS * h, ROWS * (h + 1))
             kc, ks = k_mx[g][r // 2]
             kcol = slice(P * (r % 2), P * (r % 2 + 1))
-            for b in range(QB):
-                qc, qs = q_mx[b // 2]
-                qcol = slice(P * (b % 2), P * (b % 2 + 1))
-                nc.tensor.matmul_mx(out=bank_of(k, r)[:, P * b: P * (b + 1)],
-                                    lhsT=kc[rows, kcol].bitcast(FP8X4), lhsT_scale=ks[rows, kcol],
-                                    rhs=qc[rows, qcol].bitcast(FP8X4), rhs_scale=qs[rows, qcol],
-                                    start=True, stop=True)
+            qc, qs = q_mx[b // 2]
+            qcol = slice(P * (b % 2), P * (b % 2 + 1))
+            nc.tensor.matmul_mx(out=bank_of(k, r)[:, P * b: P * (b + 1)],
+                                lhsT=kc[rows, kcol].bitcast(FP8X4), lhsT_scale=ks[rows, kcol],
+                                rhs=qc[rows, qcol].bitcast(FP8X4), rhs_scale=qs[rows, qcol],
+                                start=True, stop=True)
 
         def weights(k, r):
             col = (k // H) * PACK + r
@@ -150,25 +159,28 @@ def tile_rows_a_exp_kb_sink_kernel(tc, qT, kT, t, v, kb, sink, out):
                                  bias=bias[:, col: col + 1])
 
         def w_copy(k, i):
+            lo, hi = pieces[k][i]
             nc.vector.tensor_copy(
-                out=w_int[2 * (k % 2) + i][:].rearrange("p (c i r) -> p c r i", i=4, r=PACK),
-                in_=w_rows[k][:, :, 2 * P * i: 2 * P * (i + 1)].rearrange("p r (c i) -> p c r i", i=4))
+                out=w_int[k][i][:].rearrange("p (c i r) -> p c r i", i=4, r=PACK),
+                in_=w_rows[k][:, :, P * lo: P * hi].rearrange("p r (c i) -> p c r i", i=4))
 
         def w_quant(k, i):
-            quantize(w_mx[k][i], w_int[2 * (k % 2) + i])
+            quantize(w_mx[k][i], w_int[k][i])
 
         def pv(h, blocks, bank):
             for b in blocks:
                 for g in range(PASSES):
-                    wc, ws = w_mx[g * H + h][b // 2]
-                    wcol = slice(P * (b % 2), P * (b % 2 + 1))
+                    k = g * H + h
+                    i = [lo <= b < hi for lo, hi in pieces[k]].index(True)
+                    wc, ws = w_mx[k][i]
+                    wcol = slice(P * (b - pieces[k][i][0]), P * (b - pieces[k][i][0] + 1))
                     vcol = slice(D * g, D * (g + 1))
                     nc.tensor.matmul_mx(out=bank[:, D * b: D * (b + 1)],
                                         lhsT=wc[:, wcol].bitcast(FP8X4), lhsT_scale=ws[:, wcol],
                                         rhs=v_mx[h][0][:, vcol].bitcast(FP8X4), rhs_scale=v_mx[h][1][:, vcol],
                                         start=(g == 0), stop=(g == PASSES - 1))
 
-        parts = [(0, 0, 4, 0), (1, 0, 4, 1), (2, 0, 4, 0), (3, 0, 2, 1), (3, 2, 4, 0)]
+        parts = [(0, 0, 4, 0), (1, 0, 4, 1), (2, 0, 4, 2), (3, 0, 2, 0), (3, 2, 4, 1)]
         den = [sbuf("den%d" % i, [P, QB], F32) for i in range(len(parts))]
         rec = [sbuf("rec%d" % i, [P, QB], F32) for i in range(len(parts))]
         res = [sbuf("res%d" % i, [P, QB, D], F32) for i in range(len(parts))]
@@ -204,43 +216,93 @@ def tile_rows_a_exp_kb_sink_kernel(tc, qT, kT, t, v, kb, sink, out):
                                     in1=rec[i][:, lo:hi].unsqueeze(2).to_broadcast([P, hi - lo, D]), op=ALU.mult)
             part_store(i)
 
-        SCALAR_V = H - 1
-        prep_k1()
-        v_copy(0, nc.vector.tensor_copy)
-        v_sign(0)
-        AHEAD = 2
-        for n in range(AHEAD):
-            scores(*steps[n])
-        for n, (k, r) in enumerate(steps):
-            weights(k, r)
-            if n + AHEAD < len(steps):
-                scores(*steps[n + AHEAD])
-            if n == 12:
-                v_copy(SCALAR_V, nc.scalar.copy)
-            if r == PACK - 1 and k < H:
-                w_copy(k, 0)
-                quantize(v_mx[k], v_sg[k])
-                w_copy(k, 1)
-                w_quant(k, 0)
-                if k + 1 < H and k + 1 != SCALAR_V:
-                    v_copy(k + 1, nc.vector.tensor_copy)
-                w_quant(k, 1)
-                if k + 1 < H:
-                    v_sign(k + 1)
-        for k in range(H, TILES):
-            h = k - H
+        def v_quant(h):
+            quantize(v_mx[h], v_sg[h])
+
+        def bank_key(step):
+            return (step[0] % H, step[1] % len(banks[step[0] % H]))
+
+        slot_calls = {}
+        for m, step in enumerate(steps):
+            freed = max([-QB] + [n for n in range(m) if bank_key(steps[n]) == bank_key(step)])
+            for b in range(QB):
+                slot = max(m - 3 + b // 2, freed)
+                slot_calls.setdefault(slot, {}).setdefault(m, []).append(b)
+
+        def scores_after(slot):
+            by_step = slot_calls.get(slot, {})
+            for turn in range(QB):
+                for m in sorted(by_step):
+                    if turn < len(by_step[m]):
+                        score(steps[m][0], steps[m][1], by_step[m][turn])
+
+        def w_tile(k):
             w_copy(k, 0)
             w_copy(k, 1)
-            if h > 0:
-                part_den(h - 1)
             w_quant(k, 0)
-            if h > 0:
-                part_rec(h - 1)
-                part_scale_scalar(h - 1)
             w_quant(k, 1)
-            if h < H - 1:
-                part_pv(h)
+
+        v_copy(0)
+        quantize(k_mx[0][1], kb_bf)
+        v_sign(0)
+        v_copy(1)
+        v_quant(0)
+        v_sign(1)
+        k1_bf = [deal_pair("k_bf1%d" % i, k_raw[1], i) for i in range(2)]
+        v_quant(1)
+        quantize(k_mx[1][0], k1_bf[0])
+        quantize(k_mx[1][1], k1_bf[1])
+        v_copy(2)
+        for slot in range(-3, 0):
+            scores_after(slot)
+        for n, (k, r) in enumerate(steps):
+            weights(k, r)
+            scores_after(n)
+            if r == PACK - 1 and k == 0:
+                w_copy(0, 0)
+                v_sign(2)
+                w_copy(0, 1)
+                v_quant(2)
+                w_quant(0, 0)
+                w_quant(0, 1)
+            elif r == PACK - 1 and k == 2:
+                w_copy(2, 0)
+                w_copy(2, 1)
+                w_quant(2, 0)
+                v_copy(3)
+                w_quant(2, 1)
+                v_sign(3)
+            elif r == PACK - 1 and k == 3:
+                w_copy(3, 0)
+                v_quant(3)
+                w_copy(3, 1)
+                w_quant(3, 0)
+                w_quant(3, 1)
+            elif r == PACK - 1 and k < 6:
+                w_tile(k)
+        part_pv(0)
+        part_pv(1)
+        w_copy(6, 0)
+        w_copy(6, 1)
+        part_den(0)
+        w_quant(6, 0)
+        part_rec(0)
+        part_scale_scalar(0)
+        w_quant(6, 1)
+        part_pv(2)
+        w_copy(7, 0)
+        part_den(1)
+        w_copy(7, 1)
+        part_rec(1)
+        part_scale_scalar(1)
+        w_quant(7, 0)
         part_pv(3)
+        w_copy(7, 2)
+        part_den(2)
+        w_quant(7, 1)
+        part_rec(2)
+        part_scale_scalar(2)
+        w_quant(7, 2)
         part_pv(4)
         part_den(3)
         part_rec(3)

@@ -48,20 +48,18 @@ def tile_rows_a_exp_kb_sink_kernel(tc, qT, kT, t, v, kb, sink, out):
         nc.sync.dma_start(out=q_raw[:], in_=qT.rearrange("h (p j) n -> (h p) j n", j=PACK))
         k_view = kT.rearrange("h (p j) n -> (h p) j n", j=PACK)
         k_raw = [sbuf("k_raw%d" % g, [P, PACK, 512], F32) for g in range(PASSES)]
-        v_raw = [sbuf("v_raw%d" % h, [P, PASSES, PACK * D], F32) for h in range(H)]
+        v_raw = [sbuf("v_raw%d" % h, [P, H, PACK * D], F32) for h in range(PASSES)]
 
         def load_k(g):
             nc.sync.dma_start(out=k_raw[g][:], in_=k_view[:, :, 512 * g: 512 * (g + 1)])
 
-        def load_v(h):
-            nc.sync.dma_start(out=v_raw[h][:], in_=v[h].rearrange("(g p j) e -> p g (j e)", g=PASSES, j=PACK))
+        def load_v(g):
+            nc.sync.dma_start(out=v_raw[g][:], in_=v.rearrange("h (g p j) e -> g p h (j e)", g=PASSES, j=PACK)[g])
 
         load_k(0)
         load_v(0)
-        load_v(1)
         load_k(1)
-        load_v(2)
-        load_v(3)
+        load_v(1)
         sink_sb = sbuf("sink_sb", [P, H, QB], F32)
         nc.sync.dma_start(out=sink_sb[:], in_=sink.rearrange("h (p b) o -> p h (b o)", b=QB))
 
@@ -74,7 +72,7 @@ def tile_rows_a_exp_kb_sink_kernel(tc, qT, kT, t, v, kb, sink, out):
         b1 = sbuf("b1", [P, W8], F32)
         ln_m = sbuf("ln_m", [P, W8], F32)
         bias = sbuf("bias", [P, W8], F32)
-        sgn = sbuf("sgn", [P, W8], BF16)
+        sgn = sbuf("sgn", [P, W8], F32)
         t_bits = t_sb[:].bitcast(I32)
         nc.vector.tensor_scalar(out=pow2[:], in0=t_bits, scalar1=-(1 << 23), scalar2=None, op0=ALU.bitwise_and)
         nc.vector.tensor_scalar(out=expo[:], in0=t_bits, scalar1=23, scalar2=255,
@@ -103,28 +101,32 @@ def tile_rows_a_exp_kb_sink_kernel(tc, qT, kT, t, v, kb, sink, out):
         quantize(k_mx[0][0], ka)
         kb_bf = deal_pair("k_bf01", k_raw[0], 1)
 
-        v_mx = [planes("v%d" % h, PASSES * D) for h in range(H)]
-        v_bf = [sbuf("v_bf%d" % h, [P, PASSES * D * PACK], BF16) for h in range(H)]
-        v_sg = [sbuf("v_sg%d" % h, [P, PASSES * D * PACK], BF16) for h in range(H)]
+        def interleave(copy, dst, rows):
+            copy(out=dst[:].rearrange("p (c i r) -> p c r i", i=4, r=PACK),
+                 in_=rows.rearrange("p r (c i) -> p c r i", i=4))
 
-        def v_copy(h):
-            nc.vector.tensor_copy(
-                out=v_bf[h][:].rearrange("p (g c i j) -> p g c j i", g=PASSES, i=4, j=PACK),
-                in_=v_raw[h][:].rearrange("p g (j c i) -> p g c j i", j=PACK, i=4))
+        v_mx = [[planes("v%d%d" % (g, i), 2 * D) for i in range(2)] for g in range(PASSES)]
+        v_rows = [sbuf("v_rows%d" % g, [P, PACK, H * D], BF16) for g in range(PASSES)]
+        v_int = [[sbuf("v_int%d%d" % (g, i), [P, 2 * D * PACK], BF16) for i in range(2)] for g in range(PASSES)]
 
-        def v_sign(h):
-            nc.vector.tensor_tensor(
-                out=v_sg[h][:].rearrange("p (g e j) -> p g e j", g=PASSES, j=PACK),
-                in0=v_bf[h][:].rearrange("p (g e j) -> p g e j", g=PASSES, j=PACK),
-                in1=sgn[:].rearrange("p (g j) -> p g j", g=PASSES).unsqueeze(2).to_broadcast([P, PASSES, D, PACK]),
-                op=ALU.mult)
+        def v_sign(g):
+            for j in range(PACK):
+                nc.vector.tensor_scalar(out=v_rows[g][:, j, :].rearrange("p (h e) -> p h e", h=H),
+                                        in0=v_raw[g][:, :, D * j: D * (j + 1)],
+                                        scalar1=sgn[:, PACK * g + j: PACK * g + j + 1], scalar2=None, op0=ALU.mult)
+
+        def v_pack(g):
+            for i in range(2):
+                interleave(nc.vector.tensor_copy, v_int[g][i], v_rows[g][:, :, 2 * D * i: 2 * D * (i + 1)])
+            for i in range(2):
+                quantize(v_mx[g][i], v_int[g][i])
 
         TILES = PASSES * H
         banks = [[ps.tile([P, NQ], F32, name="s%d%d" % (h, i)) for i in range(2 if h == H - 1 else 1)]
                  for h in range(H)]
         y_bank = [ps.tile([P, NQ], F32, name="y%d" % i) for i in range(3)]
         w_rows = [sbuf("w_rows%d" % k, [P, PACK, NQ], BF16) for k in range(TILES)]
-        pieces = [[(0, 2), (2, 4)]] * (TILES - 1) + [[(0, 2), (2, 3), (3, 4)]]
+        pieces = [[(0, 2), (2, 3), (3, 4)] if k == TILES - 2 else [(0, 2), (2, 4)] for k in range(TILES)]
         w_int = [[sbuf("w_int%d%d" % (k, i), [P, (hi - lo) * P * PACK], BF16) for i, (lo, hi) in enumerate(pieces[k])]
                  for k in range(TILES)]
         w_mx = [[planes("w%d%d" % (k, i), (hi - lo) * P) for i, (lo, hi) in enumerate(pieces[k])]
@@ -158,11 +160,9 @@ def tile_rows_a_exp_kb_sink_kernel(tc, qT, kT, t, v, kb, sink, out):
             nc.scalar.activation(out=w_rows[k][:, r, :], in_=bank_of(k, r)[:], func=ACT.Exp,
                                  bias=bias[:, col: col + 1])
 
-        def w_copy(k, i):
+        def w_copy(k, i, copy=nc.vector.tensor_copy):
             lo, hi = pieces[k][i]
-            nc.vector.tensor_copy(
-                out=w_int[k][i][:].rearrange("p (c i r) -> p c r i", i=4, r=PACK),
-                in_=w_rows[k][:, :, P * lo: P * hi].rearrange("p r (c i) -> p c r i", i=4))
+            interleave(copy, w_int[k][i], w_rows[k][:, :, P * lo: P * hi])
 
         def w_quant(k, i):
             quantize(w_mx[k][i], w_int[k][i])
@@ -174,13 +174,14 @@ def tile_rows_a_exp_kb_sink_kernel(tc, qT, kT, t, v, kb, sink, out):
                     i = [lo <= b < hi for lo, hi in pieces[k]].index(True)
                     wc, ws = w_mx[k][i]
                     wcol = slice(P * (b - pieces[k][i][0]), P * (b - pieces[k][i][0] + 1))
-                    vcol = slice(D * g, D * (g + 1))
+                    vc, vs = v_mx[g][h // 2]
+                    vcol = slice(D * (h % 2), D * (h % 2 + 1))
                     nc.tensor.matmul_mx(out=bank[:, D * b: D * (b + 1)],
                                         lhsT=wc[:, wcol].bitcast(FP8X4), lhsT_scale=ws[:, wcol],
-                                        rhs=v_mx[h][0][:, vcol].bitcast(FP8X4), rhs_scale=v_mx[h][1][:, vcol],
+                                        rhs=vc[:, vcol].bitcast(FP8X4), rhs_scale=vs[:, vcol],
                                         start=(g == 0), stop=(g == PASSES - 1))
 
-        parts = [(0, 0, 4, 0), (1, 0, 4, 1), (2, 0, 4, 2), (3, 0, 2, 0), (3, 2, 4, 1)]
+        parts = [(0, 0, 4, 0), (1, 0, 4, 1), (3, 0, 4, 2), (2, 0, 2, 0), (2, 2, 4, 1)]
         den = [sbuf("den%d" % i, [P, QB], F32) for i in range(len(parts))]
         rec = [sbuf("rec%d" % i, [P, QB], F32) for i in range(len(parts))]
         res = [sbuf("res%d" % i, [P, QB, D], F32) for i in range(len(parts))]
@@ -216,9 +217,6 @@ def tile_rows_a_exp_kb_sink_kernel(tc, qT, kT, t, v, kb, sink, out):
                                     in1=rec[i][:, lo:hi].unsqueeze(2).to_broadcast([P, hi - lo, D]), op=ALU.mult)
             part_store(i)
 
-        def v_quant(h):
-            quantize(v_mx[h], v_sg[h])
-
         def bank_key(step):
             return (step[0] % H, step[1] % len(banks[step[0] % H]))
 
@@ -242,67 +240,44 @@ def tile_rows_a_exp_kb_sink_kernel(tc, qT, kT, t, v, kb, sink, out):
             w_quant(k, 0)
             w_quant(k, 1)
 
-        v_copy(0)
         quantize(k_mx[0][1], kb_bf)
         v_sign(0)
-        v_copy(1)
-        v_quant(0)
-        v_sign(1)
+        v_pack(0)
         k1_bf = [deal_pair("k_bf1%d" % i, k_raw[1], i) for i in range(2)]
-        v_quant(1)
-        quantize(k_mx[1][0], k1_bf[0])
-        quantize(k_mx[1][1], k1_bf[1])
-        v_copy(2)
+        for i in range(2):
+            quantize(k_mx[1][i], k1_bf[i])
+        v_sign(1)
+        v_pack(1)
         for slot in range(-3, 0):
             scores_after(slot)
         for n, (k, r) in enumerate(steps):
             weights(k, r)
             scores_after(n)
-            if r == PACK - 1 and k == 0:
-                w_copy(0, 0)
-                v_sign(2)
-                w_copy(0, 1)
-                v_quant(2)
-                w_quant(0, 0)
-                w_quant(0, 1)
-            elif r == PACK - 1 and k == 2:
-                w_copy(2, 0)
-                w_copy(2, 1)
-                w_quant(2, 0)
-                v_copy(3)
-                w_quant(2, 1)
-                v_sign(3)
-            elif r == PACK - 1 and k == 3:
-                w_copy(3, 0)
-                v_quant(3)
-                w_copy(3, 1)
-                w_quant(3, 0)
-                w_quant(3, 1)
-            elif r == PACK - 1 and k < 6:
+            if r == PACK - 1 and k < 6:
                 w_tile(k)
+        w_copy(7, 0, nc.scalar.copy)
+        w_copy(7, 1, nc.scalar.copy)
         part_pv(0)
         part_pv(1)
-        w_copy(6, 0)
-        w_copy(6, 1)
         part_den(0)
-        w_quant(6, 0)
+        w_quant(7, 0)
         part_rec(0)
         part_scale_scalar(0)
-        w_quant(6, 1)
-        part_pv(2)
-        w_copy(7, 0)
+        w_copy(6, 0)
         part_den(1)
-        w_copy(7, 1)
+        w_quant(7, 1)
+        part_pv(2)
         part_rec(1)
         part_scale_scalar(1)
-        w_quant(7, 0)
+        w_copy(6, 1)
+        w_quant(6, 0)
         part_pv(3)
-        w_copy(7, 2)
+        w_copy(6, 2)
         part_den(2)
-        w_quant(7, 1)
+        w_quant(6, 1)
         part_rec(2)
         part_scale_scalar(2)
-        w_quant(7, 2)
+        w_quant(6, 2)
         part_pv(4)
         part_den(3)
         part_rec(3)

@@ -17,9 +17,28 @@ ALU = mybir.AluOpType
 P = 128
 PACK = 4
 ROWS = 32
-PASSES = N // (P * PACK)
+PASS = P * PACK
+PASSES = N // PASS
+SLOTS = PASSES * PACK
 QB = NQ // P
+WIDE = 512
+GAP = WIDE - D
+TILES = PASSES * H
+RUN = 4
 LN2 = 0.6931471805599453
+AHEAD = 2
+EARLY_FROM = 16
+
+
+def step_order():
+    left = sorted([(k, r) for k in range(TILES) for r in range(PACK)], key=lambda kr: 4 * kr[0] + 3 * kr[1])
+    steps = []
+    for n in range(len(left)):
+        recent = [k % H for k, r in steps[-2:]]
+        step = ([kr for kr in left if kr[0] % H not in recent] + left)[0]
+        steps.append(step)
+        left.remove(step)
+    return steps
 
 
 def tile_rows_a_exp_kb_sink_kernel(tc, qT, kT, t, v, kb, sink, out):
@@ -38,48 +57,57 @@ def tile_rows_a_exp_kb_sink_kernel(tc, qT, kT, t, v, kb, sink, out):
         def quantize(dst, src):
             nc.vector.quantize_mx(out=dst[0][:].bitcast(FP8X4), scales=dst[1][:], in_=src[:])
 
-        t_sb = sbuf("t_sb", [P, PASSES * PACK], F32)
-        kb_sb = sbuf("kb_sb", [P, PASSES * PACK], F32)
+        t_sb = sbuf("t_sb", [P, SLOTS], F32)
+        kb_sb = sbuf("kb_sb", [P, SLOTS], F32)
         nc.sync.dma_start(out=t_sb[:].rearrange("p (g j) -> p g j", g=PASSES),
-                            in_=t.rearrange("(g p j) o -> p g (j o)", g=PASSES, j=PACK))
+                          in_=t.rearrange("(g p j) o -> p g (j o)", g=PASSES, j=PACK))
         nc.scalar.dma_start(out=kb_sb[:].rearrange("p (g j) -> p g j", g=PASSES),
                             in_=kb.rearrange("(g p j) o -> p g (j o)", g=PASSES, j=PACK))
         q_raw = sbuf("q_raw", [P, PACK, NQ], F32)
         nc.sync.dma_start(out=q_raw[:], in_=qT.rearrange("h (p j) n -> (h p) j n", j=PACK))
         k_view = kT.rearrange("h (p j) n -> (h p) j n", j=PACK)
-        k_raw = [sbuf("k_raw%d" % g, [P, PACK, 512], F32) for g in range(PASSES)]
-        v_raw = [sbuf("v_raw%d" % h, [P, H, PACK * D], F32) for h in range(PASSES)]
-
-        def load_k(g):
-            nc.sync.dma_start(out=k_raw[g][:], in_=k_view[:, :, 512 * g: 512 * (g + 1)])
-
-        def load_v(g):
-            nc.sync.dma_start(out=v_raw[g][:], in_=v.rearrange("h (g p j) e -> g p h (j e)", g=PASSES, j=PACK)[g])
-
-        load_k(0)
-        load_v(0)
-        load_k(1)
-        load_v(1)
+        v_view = v.rearrange("h (g p j) e -> g p h (j e)", g=PASSES, j=PACK)
+        k_raw = [sbuf("k_raw%d" % g, [P, PACK, PASS], F32) for g in range(PASSES)]
+        v_raw = [sbuf("v_raw%d" % g, [P, H, PACK * D], F32) for g in range(PASSES)]
+        for g in range(PASSES):
+            nc.sync.dma_start(out=k_raw[g][:], in_=k_view[:, :, PASS * g: PASS * (g + 1)])
+            nc.sync.dma_start(out=v_raw[g][:], in_=v_view[g])
         sink_sb = sbuf("sink_sb", [P, H, QB], F32)
         nc.sync.dma_start(out=sink_sb[:], in_=sink.rearrange("h (p b) o -> p h (b o)", b=QB))
 
-        W8 = PASSES * PACK
-        pow2 = sbuf("pow2", [P, W8], I32)
-        expo = sbuf("expo", [P, W8], I32)
-        inv = sbuf("inv", [P, W8], F32)
-        mant = sbuf("mant", [P, W8], F32)
-        b0 = sbuf("b0", [P, W8], F32)
-        b1 = sbuf("b1", [P, W8], F32)
-        ln_m = sbuf("ln_m", [P, W8], F32)
-        bias = sbuf("bias", [P, W8], F32)
-        sgn = sbuf("sgn", [P, W8], F32)
+        v_pad = [planes("v%d" % g, (H + 1) * WIDE) for g in range(PASSES)]
+
+        def zero_words(g, first_run, end_run):
+            runs = v_pad[g][0][:].rearrange("p (n c) -> p n c", c=WIDE)
+            nc.vector.memset(runs[:, first_run:end_run, 0:GAP], 0)
+
+        def zero_scales(g):
+            runs = v_pad[g][1][:].bitcast(U32).rearrange("p (n c) -> p n c", c=WIDE // 4)
+            nc.vector.memset(runs[:, :, 0:GAP // 4], 0)
+
+        zero_words(0, 0, H + 1)
+        zero_scales(0)
+        zero_scales(1)
+        zero_words(1, 0, 2)
+
+        pow2 = sbuf("pow2", [P, SLOTS], I32)
+        expo = sbuf("expo", [P, SLOTS], I32)
+        inv_pow2 = sbuf("inv_pow2", [P, SLOTS], F32)
+        mant = sbuf("mant", [P, SLOTS], F32)
+        e_ln2 = sbuf("e_ln2", [P, SLOTS], F32)
+        kb_e = sbuf("kb_e", [P, SLOTS], F32)
+        ln_m = sbuf("ln_m", [P, SLOTS], F32)
+        bias = sbuf("bias", [P, SLOTS], F32)
+        sgn = sbuf("sgn", [P, SLOTS], F32)
         t_bits = t_sb[:].bitcast(I32)
         nc.vector.tensor_scalar(out=pow2[:], in0=t_bits, scalar1=-(1 << 23), scalar2=None, op0=ALU.bitwise_and)
         nc.vector.tensor_scalar(out=expo[:], in0=t_bits, scalar1=23, scalar2=255,
                                 op0=ALU.logical_shift_right, op1=ALU.bitwise_and)
-        nc.vector.reciprocal(out=inv[:], in_=pow2[:].bitcast(F32))
-        nc.vector.tensor_scalar(out=b0[:], in0=expo[:], scalar1=-127.0, scalar2=LN2, op0=ALU.add, op1=ALU.mult)
-        nc.vector.tensor_tensor(out=mant[:], in0=t_sb[:], in1=inv[:], op=ALU.mult)
+        zero_words(1, 2, 4)
+        nc.vector.reciprocal(out=inv_pow2[:], in_=pow2[:].bitcast(F32))
+        nc.vector.tensor_scalar(out=e_ln2[:], in0=expo[:], scalar1=-127.0, scalar2=LN2, op0=ALU.add, op1=ALU.mult)
+        zero_words(1, 4, H + 1)
+        nc.vector.tensor_tensor(out=mant[:], in0=t_sb[:], in1=inv_pow2[:], op=ALU.mult)
         nc.scalar.activation(out=ln_m[:], in_=mant[:], func=ACT.Ln)
         nc.scalar.activation(out=sgn[:], in_=t_sb[:], func=ACT.Sign)
 
@@ -90,75 +118,67 @@ def tile_rows_a_exp_kb_sink_kernel(tc, qT, kT, t, v, kb, sink, out):
                 in_=raw[:].rearrange("p j (s r) -> p s j r", r=PACK)[:, :, :, 2 * pair: 2 * pair + 2])
             return dst
 
-        q_mx = [planes("q%d" % i, 2 * P) for i in range(2)]
+        q_mx = planes("q", NQ)
+        q_half = [(q_mx[0][:, 2 * P * i: 2 * P * (i + 1)], q_mx[1][:, 2 * P * i: 2 * P * (i + 1)]) for i in range(2)]
         k_mx = [[planes("k%d%d" % (g, i), 2 * P) for i in range(2)] for g in range(PASSES)]
         q_bf = [deal_pair("q_bf%d" % i, q_raw, i) for i in range(2)]
-        quantize(q_mx[0], q_bf[0])
-        nc.vector.tensor_tensor(out=b1[:], in0=b0[:], in1=kb_sb[:], op=ALU.add)
-        quantize(q_mx[1], q_bf[1])
-        ka = deal_pair("k_bf00", k_raw[0], 0)
-        nc.vector.tensor_tensor(out=bias[:], in0=b1[:], in1=ln_m[:], op=ALU.add)
-        quantize(k_mx[0][0], ka)
-        kb_bf = deal_pair("k_bf01", k_raw[0], 1)
+        quantize(q_half[0], q_bf[0])
+        nc.vector.tensor_tensor(out=kb_e[:], in0=e_ln2[:], in1=kb_sb[:], op=ALU.add)
+        quantize(q_half[1], q_bf[1])
+        k_first = deal_pair("k_bf00", k_raw[0], 0)
+        nc.vector.tensor_tensor(out=bias[:], in0=kb_e[:], in1=ln_m[:], op=ALU.add)
+        quantize(k_mx[0][0], k_first)
+        quantize(k_mx[0][1], deal_pair("k_bf01", k_raw[0], 1))
 
         def interleave(copy, dst, rows):
-            copy(out=dst[:].rearrange("p (c i r) -> p c r i", i=4, r=PACK),
-                 in_=rows.rearrange("p r (c i) -> p c r i", i=4))
+            copy(out=dst[:].rearrange("p (c i r) -> p c r i", i=RUN, r=PACK),
+                 in_=rows.rearrange("p r (c i) -> p c r i", i=RUN))
 
-        v_mx = [[planes("v%d%d" % (g, i), 2 * D) for i in range(2)] for g in range(PASSES)]
         v_rows = [sbuf("v_rows%d" % g, [P, PACK, H * D], BF16) for g in range(PASSES)]
         v_int = [[sbuf("v_int%d%d" % (g, i), [P, 2 * D * PACK], BF16) for i in range(2)] for g in range(PASSES)]
 
         def v_sign(g):
-            for j in range(PACK):
-                nc.vector.tensor_scalar(out=v_rows[g][:, j, :].rearrange("p (h e) -> p h e", h=H),
-                                        in0=v_raw[g][:, :, D * j: D * (j + 1)],
-                                        scalar1=sgn[:, PACK * g + j: PACK * g + j + 1], scalar2=None, op0=ALU.mult)
+            for r in range(PACK):
+                nc.vector.tensor_scalar(out=v_rows[g][:, r, :].rearrange("p (h e) -> p h e", h=H),
+                                        in0=v_raw[g][:, :, D * r: D * (r + 1)],
+                                        scalar1=sgn[:, PACK * g + r: PACK * g + r + 1], scalar2=None, op0=ALU.mult)
 
         def v_pack(g):
             for i in range(2):
                 interleave(nc.vector.tensor_copy, v_int[g][i], v_rows[g][:, :, 2 * D * i: 2 * D * (i + 1)])
-            for i in range(2):
-                quantize(v_mx[g][i], v_int[g][i])
+            for h in range(H):
+                cols = slice(WIDE * h + GAP, WIDE * (h + 1))
+                quantize((v_pad[g][0][:, cols], v_pad[g][1][:, cols]),
+                         v_int[g][h // 2][:, D * PACK * (h % 2): D * PACK * (h % 2 + 1)])
 
-        TILES = PASSES * H
-        banks = [[ps.tile([P, NQ], F32, name="s%d%d" % (h, i)) for i in range(2 if h == H - 1 else 1)]
+        banks = [[ps.tile([P, WIDE], F32, name="s%d%d" % (h, i)) for i in range(2 if h == H - 1 else 1)]
                  for h in range(H)]
-        y_bank = [ps.tile([P, NQ], F32, name="y%d" % i) for i in range(3)]
+        y_bank = [ps.tile([P, WIDE], F32, name="y%d" % i) for i in range(3)]
         w_rows = [sbuf("w_rows%d" % k, [P, PACK, NQ], BF16) for k in range(TILES)]
-        pieces = [[(0, 2), (2, 3), (3, 4)] if k == TILES - 2 else [(0, 2), (2, 4)] for k in range(TILES)]
+        pieces = [[(0, 2), (2, 3), (3, 4)] if k == TILES - 1 else [(0, 2), (2, 4)] for k in range(TILES)]
         w_int = [[sbuf("w_int%d%d" % (k, i), [P, (hi - lo) * P * PACK], BF16) for i, (lo, hi) in enumerate(pieces[k])]
                  for k in range(TILES)]
         w_mx = [[planes("w%d%d" % (k, i), (hi - lo) * P) for i, (lo, hi) in enumerate(pieces[k])]
                 for k in range(TILES)]
-        left = sorted([(k, r) for k in range(TILES) for r in range(PACK)], key=lambda kr: 4 * kr[0] + 3 * kr[1])
-        steps = []
-        for n in range(len(left)):
-            recent = [k % H for k, r in steps[-2:]]
-            step = ([kr for kr in left if kr[0] % H not in recent] + left)[0]
-            steps.append(step)
-            left.remove(step)
 
         def bank_of(k, r):
             own = banks[k % H]
             return own[r % len(own)]
 
-        def score(k, r, b):
+        def scores(k, r):
             g, h = divmod(k, H)
             rows = slice(ROWS * h, ROWS * (h + 1))
-            kc, ks = k_mx[g][r // 2]
-            kcol = slice(P * (r % 2), P * (r % 2 + 1))
-            qc, qs = q_mx[b // 2]
-            qcol = slice(P * (b % 2), P * (b % 2 + 1))
-            nc.tensor.matmul_mx(out=bank_of(k, r)[:, P * b: P * (b + 1)],
-                                lhsT=kc[rows, kcol].bitcast(FP8X4), lhsT_scale=ks[rows, kcol],
-                                rhs=qc[rows, qcol].bitcast(FP8X4), rhs_scale=qs[rows, qcol],
+            k_words, k_scales = k_mx[g][r // 2]
+            cols = slice(P * (r % 2), P * (r % 2 + 1))
+            nc.tensor.matmul_mx(out=bank_of(k, r)[:],
+                                lhsT=k_words[rows, cols].bitcast(FP8X4), lhsT_scale=k_scales[rows, cols],
+                                rhs=q_mx[0][rows, :].bitcast(FP8X4), rhs_scale=q_mx[1][rows, :],
                                 start=True, stop=True)
 
         def weights(k, r):
-            col = (k // H) * PACK + r
+            slot = (k // H) * PACK + r
             nc.scalar.activation(out=w_rows[k][:, r, :], in_=bank_of(k, r)[:], func=ACT.Exp,
-                                 bias=bias[:, col: col + 1])
+                                 bias=bias[:, slot: slot + 1])
 
         def w_copy(k, i, copy=nc.vector.tensor_copy):
             lo, hi = pieces[k][i]
@@ -167,118 +187,103 @@ def tile_rows_a_exp_kb_sink_kernel(tc, qT, kT, t, v, kb, sink, out):
         def w_quant(k, i):
             quantize(w_mx[k][i], w_int[k][i])
 
-        def pv(h, blocks, bank):
-            for b in blocks:
-                for g in range(PASSES):
-                    k = g * H + h
-                    i = [lo <= b < hi for lo, hi in pieces[k]].index(True)
-                    wc, ws = w_mx[k][i]
-                    wcol = slice(P * (b - pieces[k][i][0]), P * (b - pieces[k][i][0] + 1))
-                    vc, vs = v_mx[g][h // 2]
-                    vcol = slice(D * (h % 2), D * (h % 2 + 1))
-                    nc.tensor.matmul_mx(out=bank[:, D * b: D * (b + 1)],
-                                        lhsT=wc[:, wcol].bitcast(FP8X4), lhsT_scale=ws[:, wcol],
-                                        rhs=vc[:, vcol].bitcast(FP8X4), rhs_scale=vs[:, vcol],
-                                        start=(g == 0), stop=(g == PASSES - 1))
-
-        parts = [(0, 0, 4, 0), (1, 0, 4, 1), (3, 0, 4, 2), (2, 0, 2, 0), (2, 2, 4, 1)]
+        parts = [(0, 0, QB, 0), (1, 0, QB, 1), (2, 0, QB, 2), (3, 0, 2, 0), (3, 2, QB, 1)]
         den = [sbuf("den%d" % i, [P, QB], F32) for i in range(len(parts))]
         rec = [sbuf("rec%d" % i, [P, QB], F32) for i in range(len(parts))]
         res = [sbuf("res%d" % i, [P, QB, D], F32) for i in range(len(parts))]
 
-        def part_pv(i):
-            h, lo, hi, bk = parts[i]
-            pv(h, range(lo, hi), y_bank[bk])
+        def part_pv(i, g, blocks=None):
+            h, lo, hi, bank = parts[i]
+            k = g * H + h
+            for b in blocks or range(lo, hi):
+                piece = [first <= b < end for first, end in pieces[k]].index(True)
+                w_words, w_scales = w_mx[k][piece]
+                w_cols = slice(P * (b - pieces[k][piece][0]), P * (b - pieces[k][piece][0] + 1))
+                window = slice(WIDE * h + GAP - D * b, WIDE * (h + 1) + GAP - D * b)
+                nc.tensor.matmul_mx(out=y_bank[bank][:],
+                                    lhsT=w_words[:, w_cols].bitcast(FP8X4), lhsT_scale=w_scales[:, w_cols],
+                                    rhs=v_pad[g][0][:, window].bitcast(FP8X4), rhs_scale=v_pad[g][1][:, window],
+                                    start=(g == 0 and b == lo), stop=(g == PASSES - 1 and b == hi - 1))
 
         def part_den(i):
-            h, lo, hi, bk = parts[i]
-            y = y_bank[bk][:].rearrange("p (b e) -> p b e", e=D)
+            h, lo, hi, bank = parts[i]
+            y = y_bank[bank][:].rearrange("p (b e) -> p b e", e=D)
             nc.vector.tensor_tensor(out=den[i][:, lo:hi], in0=y[:, lo:hi, D - 1], in1=sink_sb[:, h, lo:hi], op=ALU.add)
 
         def part_rec(i):
-            h, lo, hi, bk = parts[i]
+            h, lo, hi, bank = parts[i]
             nc.vector.reciprocal(out=rec[i][:, lo:hi], in_=den[i][:, lo:hi])
 
         def part_store(i):
-            h, lo, hi, bk = parts[i]
+            h, lo, hi, bank = parts[i]
             nc.sync.dma_start(out=out[h].rearrange("(p b) e -> p b e", b=QB)[:, lo:hi, :], in_=res[i][:, lo:hi, :])
 
         def part_scale_scalar(i):
-            h, lo, hi, bk = parts[i]
+            h, lo, hi, bank = parts[i]
             for b in range(lo, hi):
-                nc.scalar.activation(out=res[i][:, b, :], in_=y_bank[bk][:, D * b: D * (b + 1)], func=ACT.Copy,
+                nc.scalar.activation(out=res[i][:, b, :], in_=y_bank[bank][:, D * b: D * (b + 1)], func=ACT.Copy,
                                      scale=rec[i][:, b: b + 1])
             part_store(i)
 
         def part_scale_vector(i):
-            h, lo, hi, bk = parts[i]
-            y = y_bank[bk][:].rearrange("p (b e) -> p b e", e=D)
+            h, lo, hi, bank = parts[i]
+            y = y_bank[bank][:].rearrange("p (b e) -> p b e", e=D)
             nc.vector.tensor_tensor(out=res[i][:, lo:hi, :], in0=y[:, lo:hi, :],
                                     in1=rec[i][:, lo:hi].unsqueeze(2).to_broadcast([P, hi - lo, D]), op=ALU.mult)
             part_store(i)
 
-        def bank_key(step):
-            return (step[0] % H, step[1] % len(banks[step[0] % H]))
-
-        slot_calls = {}
-        for m, step in enumerate(steps):
-            freed = max([-QB] + [n for n in range(m) if bank_key(steps[n]) == bank_key(step)])
-            for b in range(QB):
-                slot = max(m - 3 + b // 2, freed)
-                slot_calls.setdefault(slot, {}).setdefault(m, []).append(b)
-
-        def scores_after(slot):
-            by_step = slot_calls.get(slot, {})
-            for turn in range(QB):
-                for m in sorted(by_step):
-                    if turn < len(by_step[m]):
-                        score(steps[m][0], steps[m][1], by_step[m][turn])
-
-        def w_tile(k):
-            w_copy(k, 0)
-            w_copy(k, 1)
-            w_quant(k, 0)
-            w_quant(k, 1)
-
-        quantize(k_mx[0][1], kb_bf)
         v_sign(0)
         v_pack(0)
-        k1_bf = [deal_pair("k_bf1%d" % i, k_raw[1], i) for i in range(2)]
+        k_second = [deal_pair("k_bf1%d" % i, k_raw[1], i) for i in range(2)]
         for i in range(2):
-            quantize(k_mx[1][i], k1_bf[i])
+            quantize(k_mx[1][i], k_second[i])
         v_sign(1)
-        v_pack(1)
-        for slot in range(-3, 0):
-            scores_after(slot)
+
+        steps = step_order()
+        early = {EARLY_FROM + 2 * i: (i // 2, [2 * (i % 2), 2 * (i % 2) + 1]) for i in range(2 * len(y_bank))}
+        last, before_last = TILES - 1, TILES - 2
+        for n in range(AHEAD):
+            scores(*steps[n])
         for n, (k, r) in enumerate(steps):
             weights(k, r)
-            scores_after(n)
-            if r == PACK - 1 and k < 6:
-                w_tile(k)
-        w_copy(7, 0, nc.scalar.copy)
-        w_copy(7, 1, nc.scalar.copy)
-        part_pv(0)
-        part_pv(1)
+            if n + AHEAD < len(steps):
+                scores(*steps[n + AHEAD])
+            if n in early:
+                part_pv(early[n][0], 0, early[n][1])
+            if r == PACK - 1 and k < before_last:
+                w_copy(k, 0)
+                w_copy(k, 1)
+                w_quant(k, 0)
+                w_quant(k, 1)
+                if k == len(y_bank) - 1:
+                    v_pack(1)
+
+        w_copy(last, 0, nc.scalar.copy)
+        part_pv(0, 1)
+        part_pv(1, 1)
+        w_copy(before_last, 0)
         part_den(0)
-        w_quant(7, 0)
+        w_copy(before_last, 1)
         part_rec(0)
         part_scale_scalar(0)
-        w_copy(6, 0)
+        w_quant(before_last, 0)
         part_den(1)
-        w_quant(7, 1)
-        part_pv(2)
+        w_quant(before_last, 1)
         part_rec(1)
         part_scale_scalar(1)
-        w_copy(6, 1)
-        w_quant(6, 0)
-        part_pv(3)
-        w_copy(6, 2)
+        part_pv(2, 1)
+        part_pv(3, 0)
+        part_pv(4, 0)
+        w_copy(last, 1)
+        w_quant(last, 0)
+        w_copy(last, 2)
         part_den(2)
-        w_quant(6, 1)
+        w_quant(last, 1)
         part_rec(2)
         part_scale_scalar(2)
-        w_quant(6, 2)
-        part_pv(4)
+        w_quant(last, 2)
+        part_pv(3, 1)
+        part_pv(4, 1)
         part_den(3)
         part_rec(3)
         part_scale_scalar(3)

from contextlib import ExitStack

import concourse.mybir as mybir

H, D, NQ, N = 4, 128, 512, 1024
FLOPS = 2 * 2 * H * NQ * N * D

F32 = mybir.dt.float32
BF16 = mybir.dt.bfloat16
I32 = mybir.dt.int32
U32 = mybir.dt.uint32
U8 = mybir.dt.uint8
FP8X4 = mybir.dt.float8_e4m3fn_x4
ACT = mybir.ActivationFunctionType
ALU = mybir.AluOpType

P = 128
PACK = 4
ROWS = 32
PASS = P * PACK
PASSES = N // PASS
SLOTS = PASSES * PACK
QB = NQ // P
WIDE = 512
GAP = WIDE - D
TILES = PASSES * H
RUN = 4
LN2 = 0.6931471805599453
AHEAD = 2
EARLY_FROM = 16


def step_order():
    left = sorted([(k, r) for k in range(TILES) for r in range(PACK)], key=lambda kr: 4 * kr[0] + 3 * kr[1])
    steps = []
    for n in range(len(left)):
        recent = [k % H for k, r in steps[-2:]]
        step = ([kr for kr in left if kr[0] % H not in recent] + left)[0]
        steps.append(step)
        left.remove(step)
    return steps


def tile_rows_a_exp_kb_sink_kernel(tc, qT, kT, t, v, kb, sink, out):
    nc = tc.nc
    with ExitStack() as ctx:
        sb = ctx.enter_context(tc.tile_pool(name="sb", bufs=1))
        ps = ctx.enter_context(tc.psum_pool(name="ps", bufs=1))
        ctx.enter_context(tc.manual_schedule())

        def sbuf(name, shape, dtype):
            return sb.tile(shape, dtype, name=name, align_bytes=64)

        def planes(name, width):
            return sbuf(name + "_c", [P, width], U32), sbuf(name + "_s", [P, width], U8)

        def quantize(dst, src):
            nc.vector.quantize_mx(out=dst[0][:].bitcast(FP8X4), scales=dst[1][:], in_=src[:])

        t_sb = sbuf("t_sb", [P, SLOTS], F32)
        kb_sb = sbuf("kb_sb", [P, SLOTS], F32)
        nc.sync.dma_start(out=t_sb[:].rearrange("p (g j) -> p g j", g=PASSES),
                          in_=t.rearrange("(g p j) o -> p g (j o)", g=PASSES, j=PACK))
        nc.scalar.dma_start(out=kb_sb[:].rearrange("p (g j) -> p g j", g=PASSES),
                            in_=kb.rearrange("(g p j) o -> p g (j o)", g=PASSES, j=PACK))
        q_raw = sbuf("q_raw", [P, PACK, NQ], F32)
        nc.sync.dma_start(out=q_raw[:], in_=qT.rearrange("h (p j) n -> (h p) j n", j=PACK))
        k_view = kT.rearrange("h (p j) n -> (h p) j n", j=PACK)
        v_view = v.rearrange("h (g p j) e -> g p h (j e)", g=PASSES, j=PACK)
        k_raw = [sbuf("k_raw%d" % g, [P, PACK, PASS], F32) for g in range(PASSES)]
        v_raw = [sbuf("v_raw%d" % g, [P, H, PACK * D], F32) for g in range(PASSES)]
        for g in range(PASSES):
            nc.sync.dma_start(out=k_raw[g][:], in_=k_view[:, :, PASS * g: PASS * (g + 1)])
            nc.sync.dma_start(out=v_raw[g][:], in_=v_view[g])
        sink_sb = sbuf("sink_sb", [P, H, QB], F32)
        nc.sync.dma_start(out=sink_sb[:], in_=sink.rearrange("h (p b) o -> p h (b o)", b=QB))

        v_pad = [planes("v%d" % g, (H + 1) * WIDE) for g in range(PASSES)]

        def zero_words(g, first_run, end_run):
            runs = v_pad[g][0][:].rearrange("p (n c) -> p n c", c=WIDE)
            nc.vector.memset(runs[:, first_run:end_run, 0:GAP], 0)

        def zero_scales(g):
            runs = v_pad[g][1][:].bitcast(U32).rearrange("p (n c) -> p n c", c=WIDE // 4)
            nc.vector.memset(runs[:, :, 0:GAP // 4], 0)

        zero_words(0, 0, H + 1)
        zero_scales(0)
        zero_scales(1)
        zero_words(1, 0, 2)

        pow2 = sbuf("pow2", [P, SLOTS], I32)
        expo = sbuf("expo", [P, SLOTS], I32)
        inv_pow2 = sbuf("inv_pow2", [P, SLOTS], F32)
        mant = sbuf("mant", [P, SLOTS], F32)
        e_ln2 = sbuf("e_ln2", [P, SLOTS], F32)
        kb_e = sbuf("kb_e", [P, SLOTS], F32)
        ln_m = sbuf("ln_m", [P, SLOTS], F32)
        bias = sbuf("bias", [P, SLOTS], F32)
        sgn = sbuf("sgn", [P, SLOTS], F32)
        t_bits = t_sb[:].bitcast(I32)
        nc.vector.tensor_scalar(out=pow2[:], in0=t_bits, scalar1=-(1 << 23), scalar2=None, op0=ALU.bitwise_and)
        nc.vector.tensor_scalar(out=expo[:], in0=t_bits, scalar1=23, scalar2=255,
                                op0=ALU.logical_shift_right, op1=ALU.bitwise_and)
        zero_words(1, 2, 4)
        nc.vector.reciprocal(out=inv_pow2[:], in_=pow2[:].bitcast(F32))
        nc.vector.tensor_scalar(out=e_ln2[:], in0=expo[:], scalar1=-127.0, scalar2=LN2, op0=ALU.add, op1=ALU.mult)
        zero_words(1, 4, H + 1)
        nc.vector.tensor_tensor(out=mant[:], in0=t_sb[:], in1=inv_pow2[:], op=ALU.mult)
        nc.scalar.activation(out=ln_m[:], in_=mant[:], func=ACT.Ln)
        nc.scalar.activation(out=sgn[:], in_=t_sb[:], func=ACT.Sign)

        def deal_pair(name, raw, pair):
            dst = sbuf(name, [P, 2 * P * PACK], BF16)
            nc.vector.tensor_copy(
                out=dst[:].rearrange("p (r s j) -> p s j r", r=2, j=PACK),
                in_=raw[:].rearrange("p j (s r) -> p s j r", r=PACK)[:, :, :, 2 * pair: 2 * pair + 2])
            return dst

        q_mx = planes("q", NQ)
        q_half = [(q_mx[0][:, 2 * P * i: 2 * P * (i + 1)], q_mx[1][:, 2 * P * i: 2 * P * (i + 1)]) for i in range(2)]
        k_mx = [[planes("k%d%d" % (g, i), 2 * P) for i in range(2)] for g in range(PASSES)]
        q_bf = [deal_pair("q_bf%d" % i, q_raw, i) for i in range(2)]
        quantize(q_half[0], q_bf[0])
        nc.vector.tensor_tensor(out=kb_e[:], in0=e_ln2[:], in1=kb_sb[:], op=ALU.add)
        quantize(q_half[1], q_bf[1])
        k_first = deal_pair("k_bf00", k_raw[0], 0)
        nc.vector.tensor_tensor(out=bias[:], in0=kb_e[:], in1=ln_m[:], op=ALU.add)
        quantize(k_mx[0][0], k_first)
        quantize(k_mx[0][1], deal_pair("k_bf01", k_raw[0], 1))

        def interleave(copy, dst, rows):
            copy(out=dst[:].rearrange("p (c i r) -> p c r i", i=RUN, r=PACK),
                 in_=rows.rearrange("p r (c i) -> p c r i", i=RUN))

        v_rows = [sbuf("v_rows%d" % g, [P, PACK, H * D], BF16) for g in range(PASSES)]
        v_int = [[sbuf("v_int%d%d" % (g, i), [P, 2 * D * PACK], BF16) for i in range(2)] for g in range(PASSES)]

        def v_sign(g):
            for r in range(PACK):
                nc.vector.tensor_scalar(out=v_rows[g][:, r, :].rearrange("p (h e) -> p h e", h=H),
                                        in0=v_raw[g][:, :, D * r: D * (r + 1)],
                                        scalar1=sgn[:, PACK * g + r: PACK * g + r + 1], scalar2=None, op0=ALU.mult)

        def v_pack(g):
            for i in range(2):
                interleave(nc.vector.tensor_copy, v_int[g][i], v_rows[g][:, :, 2 * D * i: 2 * D * (i + 1)])
            for h in range(H):
                cols = slice(WIDE * h + GAP, WIDE * (h + 1))
                quantize((v_pad[g][0][:, cols], v_pad[g][1][:, cols]),
                         v_int[g][h // 2][:, D * PACK * (h % 2): D * PACK * (h % 2 + 1)])

        banks = [[ps.tile([P, WIDE], F32, name="s%d%d" % (h, i)) for i in range(2 if h == H - 1 else 1)]
                 for h in range(H)]
        y_bank = [ps.tile([P, WIDE], F32, name="y%d" % i) for i in range(3)]
        w_rows = [sbuf("w_rows%d" % k, [P, PACK, NQ], BF16) for k in range(TILES)]
        pieces = [[(0, 2), (2, 3), (3, 4)] if k == TILES - 1 else [(0, 2), (2, 4)] for k in range(TILES)]
        w_int = [[sbuf("w_int%d%d" % (k, i), [P, (hi - lo) * P * PACK], BF16) for i, (lo, hi) in enumerate(pieces[k])]
                 for k in range(TILES)]
        w_mx = [[planes("w%d%d" % (k, i), (hi - lo) * P) for i, (lo, hi) in enumerate(pieces[k])]
                for k in range(TILES)]

        def bank_of(k, r):
            own = banks[k % H]
            return own[r % len(own)]

        def scores(k, r):
            g, h = divmod(k, H)
            rows = slice(ROWS * h, ROWS * (h + 1))
            k_words, k_scales = k_mx[g][r // 2]
            cols = slice(P * (r % 2), P * (r % 2 + 1))
            nc.tensor.matmul_mx(out=bank_of(k, r)[:],
                                lhsT=k_words[rows, cols].bitcast(FP8X4), lhsT_scale=k_scales[rows, cols],
                                rhs=q_mx[0][rows, :].bitcast(FP8X4), rhs_scale=q_mx[1][rows, :],
                                start=True, stop=True)

        def weights(k, r):
            slot = (k // H) * PACK + r
            nc.scalar.activation(out=w_rows[k][:, r, :], in_=bank_of(k, r)[:], func=ACT.Exp,
                                 bias=bias[:, slot: slot + 1])

        def w_copy(k, i, copy=nc.vector.tensor_copy):
            lo, hi = pieces[k][i]
            interleave(copy, w_int[k][i], w_rows[k][:, :, P * lo: P * hi])

        def w_quant(k, i):
            quantize(w_mx[k][i], w_int[k][i])

        parts = [(0, 0, QB, 0), (1, 0, QB, 1), (2, 0, QB, 2), (3, 0, 2, 0), (3, 2, QB, 1)]
        den = [sbuf("den%d" % i, [P, QB], F32) for i in range(len(parts))]
        rec = [sbuf("rec%d" % i, [P, QB], F32) for i in range(len(parts))]
        res = [sbuf("res%d" % i, [P, QB, D], F32) for i in range(len(parts))]

        def part_pv(i, g, blocks=None):
            h, lo, hi, bank = parts[i]
            k = g * H + h
            for b in blocks or range(lo, hi):
                piece = [first <= b < end for first, end in pieces[k]].index(True)
                w_words, w_scales = w_mx[k][piece]
                w_cols = slice(P * (b - pieces[k][piece][0]), P * (b - pieces[k][piece][0] + 1))
                window = slice(WIDE * h + GAP - D * b, WIDE * (h + 1) + GAP - D * b)
                nc.tensor.matmul_mx(out=y_bank[bank][:],
                                    lhsT=w_words[:, w_cols].bitcast(FP8X4), lhsT_scale=w_scales[:, w_cols],
                                    rhs=v_pad[g][0][:, window].bitcast(FP8X4), rhs_scale=v_pad[g][1][:, window],
                                    start=(g == 0 and b == lo), stop=(g == PASSES - 1 and b == hi - 1))

        def part_den(i):
            h, lo, hi, bank = parts[i]
            y = y_bank[bank][:].rearrange("p (b e) -> p b e", e=D)
            nc.vector.tensor_tensor(out=den[i][:, lo:hi], in0=y[:, lo:hi, D - 1], in1=sink_sb[:, h, lo:hi], op=ALU.add)

        def part_rec(i):
            h, lo, hi, bank = parts[i]
            nc.vector.reciprocal(out=rec[i][:, lo:hi], in_=den[i][:, lo:hi])

        def part_store(i):
            h, lo, hi, bank = parts[i]
            nc.sync.dma_start(out=out[h].rearrange("(p b) e -> p b e", b=QB)[:, lo:hi, :], in_=res[i][:, lo:hi, :])

        def part_scale_scalar(i):
            h, lo, hi, bank = parts[i]
            for b in range(lo, hi):
                nc.scalar.activation(out=res[i][:, b, :], in_=y_bank[bank][:, D * b: D * (b + 1)], func=ACT.Copy,
                                     scale=rec[i][:, b: b + 1])
            part_store(i)

        def part_scale_vector(i):
            h, lo, hi, bank = parts[i]
            y = y_bank[bank][:].rearrange("p (b e) -> p b e", e=D)
            nc.vector.tensor_tensor(out=res[i][:, lo:hi, :], in0=y[:, lo:hi, :],
                                    in1=rec[i][:, lo:hi].unsqueeze(2).to_broadcast([P, hi - lo, D]), op=ALU.mult)
            part_store(i)

        v_sign(0)
        v_pack(0)
        k_second = [deal_pair("k_bf1%d" % i, k_raw[1], i) for i in range(2)]
        for i in range(2):
            quantize(k_mx[1][i], k_second[i])
        v_sign(1)

        steps = step_order()
        early = {EARLY_FROM + 2 * i: (i // 2, [2 * (i % 2), 2 * (i % 2) + 1]) for i in range(2 * len(y_bank))}
        last, before_last = TILES - 1, TILES - 2
        for n in range(AHEAD):
            scores(*steps[n])
        for n, (k, r) in enumerate(steps):
            weights(k, r)
            if n + AHEAD < len(steps):
                scores(*steps[n + AHEAD])
            if n in early:
                part_pv(early[n][0], 0, early[n][1])
            if r == PACK - 1 and k < before_last:
                w_copy(k, 0)
                w_copy(k, 1)
                w_quant(k, 0)
                w_quant(k, 1)
                if k == len(y_bank) - 1:
                    v_pack(1)

        w_copy(last, 0, nc.scalar.copy)
        part_pv(0, 1)
        part_pv(1, 1)
        w_copy(before_last, 0)
        part_den(0)
        w_copy(before_last, 1)
        part_rec(0)
        part_scale_scalar(0)
        w_quant(before_last, 0)
        part_den(1)
        w_quant(before_last, 1)
        part_rec(1)
        part_scale_scalar(1)
        part_pv(2, 1)
        part_pv(3, 0)
        part_pv(4, 0)
        w_copy(last, 1)
        w_quant(last, 0)
        w_copy(last, 2)
        part_den(2)
        w_quant(last, 1)
        part_rec(2)
        part_scale_scalar(2)
        w_quant(last, 2)
        part_pv(3, 1)
        part_pv(4, 1)
        part_den(3)
        part_rec(3)
        part_scale_scalar(3)
        part_den(4)
        part_rec(4)
        part_scale_vector(4)
